import numpy as np, ml_dtypes
CORES = [211,219,227,235,243,251,83,91,99,107,115,123]
N = 12
KB, QP = 4, 64
WB = 1
def setup_inputs(rng):
    q = rng.standard_normal((N, 128, QP), dtype=np.float32) / 4; k = rng.standard_normal((N, 128, KB * 128), dtype=np.float32)
    a = 2 * np.pi * rng.random((N, QP)); s = 400 * rng.random((N, QP)) ** 1.5; q[:, 0, :] = s * np.cos(a); q[:, 1, :] = s * np.sin(a); q[:, 2, :] = 150 * rng.standard_normal((N, QP)); k[:, 2, :] = 1 + k[:, 2, :] / 50
    a = (2 * np.pi * rng.random() + np.pi / 2 * (rng.permutation(N).reshape(N, 1, 1) + 0.5) / N - 0.5 + (np.arange(KB).reshape(1, KB, 1) + rng.random((N, KB, 128))) / KB).reshape(N, KB * 128); k[:, 0, :] = np.cos(a); k[:, 1, :] = np.sin(a)
    return {"q": q.astype(ml_dtypes.bfloat16), "k": k.astype(ml_dtypes.bfloat16), "v": rng.standard_normal((N, 128, KB * 128), dtype=np.float32).astype(ml_dtypes.bfloat16)}
def reference(q, k, v):
    Q, K, V = q.astype(np.float64), k.astype(np.float64), v.astype(np.float64)
    y = np.zeros((N, QP, 128))
    for r in range(N):
        js = list(range(max(0, r - WB), r + 1))
        S = np.concatenate([K[j].T @ Q[r] for j in js], axis=0)
        P = np.exp(S - S.max(axis=0)); P = P / P.sum(axis=0)
        y[r] = P.T @ np.concatenate([V[j][:, 128 * b:128 * b + 128] for j in js for b in range(KB)], axis=0)
    return {"y": y.astype(ml_dtypes.bfloat16)}

@@ -1,0 +1,188 @@
+from concourse.mybir import AluOpType, AxisListType, ActivationFunctionType
+
+QP, KB, BK = 64, 4, 128
+MW = QP + 2
+CLAMP = 60.0
+
+SCRATCH = {
+    "qo": ("sbuf", [128, QP], "bfloat16"), "qn": ("sbuf", [128, QP], "bfloat16"),
+    "kk": ("sbuf", [128, KB * BK], "bfloat16"), "vv": ("sbuf", [128, KB * BK], "bfloat16"),
+    "zer": ("sbuf", [128, 128], "float32"), "negbig": ("sbuf", [128, 128], "float32"),
+    "idn": ("sbuf", [128, 128], "bfloat16"),
+    "nmo": ("sbuf", [128, 2], "float32"), "negmo": ("sbuf", [128, 1], "bfloat16"),
+    "po": ("sbuf", [128, KB * BK], "bfloat16"), "l2o": ("sbuf", [128, 2], "float32"),
+    "lo": ("sbuf", [128, 1], "float32"), "pto": ("sbuf", [128, KB * QP], "bfloat16"),
+    "zo": ("sbuf", [128, 128], "bfloat16"),
+    "nms": ("sbuf", [128, KB], "float32"), "ps": ("sbuf", [128, KB * BK], "bfloat16"),
+    "l4s": ("sbuf", [128, KB], "float32"), "lfs": ("sbuf", [128, 1], "float32"),
+    "pts": ("sbuf", [128, KB * QP], "bfloat16"), "msg": ("sbuf", [128, MW], "bfloat16"),
+    "ret": ("sbuf", [128, MW], "bfloat16"), "t1": ("sbuf", [128, 1], "float32"),
+    "al": ("sbuf", [128, 1], "bfloat16"), "da": ("sbuf", [128, QP], "bfloat16"),
+    "lsum": ("sbuf", [128, 1], "float32"), "rec": ("sbuf", [128, 1], "float32"),
+    "yb": ("sbuf", [128, 128], "bfloat16"),
+}
+for _b in range(8):
+    SCRATCH["b%d" % _b] = ("psum", [128, 512], "float32")
+
+SEMAPHORES = (["z", "mz", "nb", "idr", "lq", "lk", "lv", "qarr", "qsent", "rarr", "rsent",
+               "oS0", "oS1", "orr", "om", "oe0", "oe1", "oT0", "oT1", "oc0", "oc1", "ol", "oO", "oZ",
+               "sr", "sm", "sO", "slr", "sl", "sF", "rt", "ra", "rD", "rs", "rL", "rr", "ry", "st"]
+              + ["sS%d" % c for c in range(KB)] + ["se%d" % c for c in range(KB)]
+              + ["sT%d" % c for c in range(KB)] + ["sc%d" % c for c in range(KB)])
+
+
+def rank_program(g, core, T, topo):
+    r = T.rank_of(core)
+    if r is None:
+        return
+    prev = T.cores[r - 1] if r > 0 else None
+    nxt = T.cores[r + 1] if r + 1 < len(T.cores) else None
+    S = T.sem
+    pe, dve, act, sp = g.tensor, g.vector, g.scalar, g.sync
+    Exp = ActivationFunctionType.Exp
+    X = AxisListType.X
+    Q = slice(0, QP)
+    bank = [T["b%d" % b] for b in range(8)]
+
+    def engines(mask):
+        return bin(mask).count("1")
+
+    sp.dma_start(T.qo[:], T.q[:]).then_inc(S.lq, 16)
+    sp.dma_start(T.kk[:], T.k[:]).then_inc(S.lk, 16)
+    sp.dma_start(T.vv[:], T.v[:]).then_inc(S.lv, 16)
+
+    dve.memset(T.zer[:], 0.0).then_inc(S.z, 1)
+    if nxt is not None:
+        dve.memset(T.msg[:, QP:MW], 0.0).then_inc(S.mz, 1)
+    g.wait_ge(S.z, 1)
+    g.affine_select(T.negbig[:], T.zer[:], [[-1, 128]], AluOpType.is_equal, -30000.0, 0, 1).then_inc(S.nb, 1)
+    act.wait_ge(S.nb, 1)
+    act.activation(T.idn[:], T.negbig[:], Exp).then_inc(S.idr, 1)
+
+    if prev is not None:
+        rid, pid = topo.addr(prev, core)
+        mq = topo.mask(core, prev)
+        g.wait_ge(S.lq, 16)
+        g.remote_dma(T.qn[:], T.qo[:], S.qarr, S.qsent, pid, rid, mq)
+
+    H = KB * BK // 2
+    pe.wait_ge(S.lq, 16)
+    pe.wait_ge(S.lk, 16)
+    for c in range(2):
+        pe.matmul(bank[5 + c][Q, 0:H], T.qo[:], T.kk[:, c * H:(c + 1) * H], True, True).then_inc(S["oS%d" % c], 1)
+    for c in range(2):
+        dve.wait_ge(S["oS%d" % c], 1)
+        dve.tensor_reduce(T.nmo[Q, c:c + 1], bank[5 + c][Q, 0:H], X, AluOpType.max, negate=True).then_inc(S.orr, 1)
+    dve.wait_ge(S.orr, 2)
+    dve.tensor_reduce(T.negmo[Q, :], T.nmo[Q, :], X, AluOpType.min).then_inc(S.om, 1)
+    act.wait_ge(S.om, 1)
+    for c in range(2):
+        act.activation(T.po[Q, c * H:(c + 1) * H], bank[5 + c][Q, 0:H], Exp, bias=T.negmo[Q, :], scale=1.0,
+                       accum_out=T.l2o[Q, c:c + 1]).then_inc(S["oe%d" % c], 1)
+    pe.wait_ge(S.idr, 1)
+    for c in range(2):
+        pe.wait_ge(S["oe%d" % c], 1)
+        for h in range(2):
+            b = 2 * c + h
+            pe.matmul(bank[5 + c][:, h * QP:(h + 1) * QP], T.po[Q, b * BK:(b + 1) * BK], T.idn[Q, Q],
+                      True, True).then_inc(S["oT%d" % c], 1)
+    dve.wait_ge(S.oT0, 2)
+    dve.tensor_copy(T.pto[:, 0:2 * QP], bank[5][:, 0:2 * QP]).then_inc(S.oc0, 1)
+    dve.wait_ge(S.oe0, 1)
+    dve.wait_ge(S.oe1, 1)
+    dve.tensor_reduce(T.lo[Q, :], T.l2o[Q, :], X, AluOpType.add).then_inc(S.ol, 1)
+    dve.wait_ge(S.oT1, 2)
+    dve.tensor_copy(T.pto[:, 2 * QP:4 * QP], bank[6][:, 0:2 * QP]).then_inc(S.oc1, 1)
+
+    if nxt is not None:
+        rid, pid = topo.addr(nxt, core)
+        mr = topo.mask(core, nxt)
+        pe.wait_ge(S.qarr, engines(topo.mask(nxt, core)))
+        for c in range(KB):
+            pe.matmul(bank[c][Q, 0:BK], T.qn[:], T.kk[:, c * BK:(c + 1) * BK], True, True).then_inc(S["sS%d" % c], 1)
+        for c in range(KB):
+            dve.wait_ge(S["sS%d" % c], 1)
+            dve.tensor_reduce(T.nms[Q, c:c + 1], bank[c][Q, 0:BK], X, AluOpType.max, negate=True).then_inc(S.sr, 1)
+        dve.wait_ge(S.sr, KB)
+        dve.wait_ge(S.mz, 1)
+        dve.tensor_reduce(T.msg[Q, QP + 1:QP + 2], T.nms[Q, :], X, AluOpType.min).then_inc(S.sm, 1)
+        act.wait_ge(S.sm, 1)
+        for c in range(KB):
+            act.activation(T.ps[Q, c * BK:(c + 1) * BK], bank[c][Q, 0:BK], Exp, bias=T.msg[Q, QP + 1:QP + 2], scale=1.0,
+                           accum_out=T.l4s[Q, c:c + 1]).then_inc(S["se%d" % c], 1)
+
+        def turn(c):
+            pe.wait_ge(S["se%d" % c], 1)
+            pe.matmul(bank[c][:, 0:QP], T.ps[Q, c * BK:(c + 1) * BK], T.idn[Q, Q], True, True).then_inc(S["sT%d" % c], 1)
+
+        def pv(c):
+            pe.wait_ge(S["sc%d" % c], 1)
+            i = pe.matmul(bank[4][:, 0:QP], T.vv[:, c * BK:(c + 1) * BK], T.pts[:, c * QP:(c + 1) * QP], c == 0, c == KB - 1)
+            if c == KB - 1:
+                i.then_inc(S.sO, 1)
+
+        pe.wait_ge(S.lv, 16)
+        turn(0)
+        for c in range(1, KB):
+            turn(c)
+            pv(c - 1)
+        pv(KB - 1)
+        for c in range(KB):
+            if c == KB - 1:
+                dve.wait_ge(S["se%d" % c], 1)
+                dve.tensor_reduce(T.lfs[Q, :], T.l4s[Q, :], X, AluOpType.add).then_inc(S.slr, 1)
+            dve.wait_ge(S["sT%d" % c], 1)
+            dve.tensor_copy(T.pts[:, c * QP:(c + 1) * QP], bank[c][:, 0:QP]).then_inc(S["sc%d" % c], 1)
+        dve.wait_ge(S.slr, 1)
+        dve.tensor_copy(T.msg[Q, QP:QP + 1], T.lfs[Q, :]).then_inc(S.sl, 1)
+        dve.wait_ge(S.sO, 1)
+        dve.tensor_copy(T.msg[:, 0:QP], bank[4][:, 0:QP]).then_inc(S.sF, 1)
+        g.wait_ge(S.sl, 1)
+        g.wait_ge(S.sF, 1)
+        g.remote_dma(T.ret[:], T.msg[:], S.rarr, S.rsent, pid, rid, mr)
+
+    pe.wait_ge(S.lv, 16)
+    pe.wait_ge(S.oc0, 1)
+    pe.wait_ge(S.oc1, 1)
+    for b in range(KB):
+        i = pe.matmul(bank[7][Q, 0:128], T.pto[:, b * QP:(b + 1) * QP], T.vv[:, b * BK:(b + 1) * BK], b == 0, b == KB - 1)
+    i.then_inc(S.oO, 1)
+
+    if prev is None:
+        dve.wait_ge(S.ol, 1)
+        dve.reciprocal(T.rec[Q, :], T.lo[Q, :]).then_inc(S.rr, 1)
+        dve.wait_ge(S.rr, 1)
+        dve.wait_ge(S.oO, 1)
+        dve.tensor_scalar(T.yb[Q, :], bank[7][Q, 0:128], T.rec[Q, :], None, AluOpType.mult).then_inc(S.ry, 1)
+    else:
+        dve.wait_ge(S.oO, 1)
+        dve.tensor_copy(T.zo[Q, :], bank[7][Q, 0:128]).then_inc(S.oZ, 1)
+        na = engines(topo.mask(prev, core))
+        pe.wait_ge(S.rarr, na)
+        pe.matmul(bank[5][Q, 0:128], T.ret[:, 0:QP], T.idn[:], True, False)
+        dve.wait_ge(S.rarr, na)
+        dve.tensor_scalar(T.t1[Q, :], T.ret[Q, QP + 1:QP + 2], T.negmo[Q, :], CLAMP,
+                          AluOpType.subtract, AluOpType.min).then_inc(S.rt, 1)
+        act.wait_ge(S.rt, 1)
+        act.activation(T.al[Q, :], T.t1[Q, :], Exp).then_inc(S.ra, 1)
+        act.activation(T.da[Q, :], T.negbig[Q, Q], Exp, bias=T.t1[Q, :], scale=1.0).then_inc(S.rD, 1)
+        pe.wait_ge(S.rD, 1)
+        pe.wait_ge(S.oZ, 1)
+        pe.matmul(bank[5][Q, 0:128], T.da[Q, :], T.zo[Q, :], False, True).then_inc(S.rs, 1)
+        dve.wait_ge(S.ra, 1)
+        dve.wait_ge(S.ol, 1)
+        dve.tensor_scalar(T.lsum[Q, :], T.lo[Q, :], T.al[Q, :], T.ret[Q, QP:QP + 1],
+                          AluOpType.mult, AluOpType.add).then_inc(S.rL, 1)
+        dve.wait_ge(S.rL, 1)
+        dve.reciprocal(T.rec[Q, :], T.lsum[Q, :]).then_inc(S.rr, 1)
+        dve.wait_ge(S.rr, 1)
+        dve.wait_ge(S.rs, 1)
+        dve.tensor_scalar(T.yb[Q, :], bank[5][Q, 0:128], T.rec[Q, :], None, AluOpType.mult).then_inc(S.ry, 1)
+
+    sp.wait_ge(S.ry, 1)
+    sp.dma_start(T.y[:], T.yb[Q, :]).then_inc(S.st, 16)
+    sp.wait_ge(S.st, 16)
+    if prev is not None:
+        g.wait_ge(S.qsent, engines(topo.mask(core, prev)))
+    if nxt is not None:
+        g.wait_ge(S.rsent, engines(topo.mask(core, nxt)))

@@ -1,32 +1,33 @@
 from concourse.mybir import AluOpType, AxisListType, ActivationFunctionType
 
 QP, KB, BK = 64, 4, 128
-MW = QP + 2
 CLAMP = 60.0
 
 SCRATCH = {
-    "qo": ("sbuf", [128, QP], "bfloat16"), "qn": ("sbuf", [128, QP], "bfloat16"),
+    "qo": ("sbuf", [128, QP], "bfloat16"),
     "kk": ("sbuf", [128, KB * BK], "bfloat16"), "vv": ("sbuf", [128, KB * BK], "bfloat16"),
+    "kn": ("sbuf", [128, KB * BK], "bfloat16"), "vn": ("sbuf", [128, KB * BK], "bfloat16"),
     "zer": ("sbuf", [128, 128], "float32"), "negbig": ("sbuf", [128, 128], "float32"),
     "idn": ("sbuf", [128, 128], "bfloat16"),
     "nmo": ("sbuf", [128, 2], "float32"), "negmo": ("sbuf", [128, 1], "bfloat16"),
     "po": ("sbuf", [128, KB * BK], "bfloat16"), "l2o": ("sbuf", [128, 2], "float32"),
     "lo": ("sbuf", [128, 1], "float32"), "pto": ("sbuf", [128, KB * QP], "bfloat16"),
     "zo": ("sbuf", [128, 128], "bfloat16"),
-    "nms": ("sbuf", [128, KB], "float32"), "ps": ("sbuf", [128, KB * BK], "bfloat16"),
+    "nms": ("sbuf", [128, KB], "float32"), "negms": ("sbuf", [128, 1], "bfloat16"),
+    "ps": ("sbuf", [128, KB * BK], "bfloat16"),
     "l4s": ("sbuf", [128, KB], "float32"), "lfs": ("sbuf", [128, 1], "float32"),
-    "pts": ("sbuf", [128, KB * QP], "bfloat16"), "msg": ("sbuf", [128, MW], "bfloat16"),
-    "ret": ("sbuf", [128, MW], "bfloat16"), "t1": ("sbuf", [128, 1], "float32"),
-    "al": ("sbuf", [128, 1], "bfloat16"), "da": ("sbuf", [128, QP], "bfloat16"),
+    "pts": ("sbuf", [128, KB * QP], "bfloat16"), "ot": ("sbuf", [128, QP], "bfloat16"),
+    "t1": ("sbuf", [128, 1], "float32"),
+    "al": ("sbuf", [128, 1], "float32"), "da": ("sbuf", [128, QP], "bfloat16"),
     "lsum": ("sbuf", [128, 1], "float32"), "rec": ("sbuf", [128, 1], "float32"),
     "yb": ("sbuf", [128, 128], "bfloat16"),
 }
 for _b in range(8):
     SCRATCH["b%d" % _b] = ("psum", [128, 512], "float32")
 
-SEMAPHORES = (["z", "mz", "nb", "idr", "lq", "lk", "lv", "qarr", "qsent", "rarr", "rsent",
+SEMAPHORES = (["z", "nb", "idr", "lq", "lk", "lv", "karr", "varr", "ksent", "vsent",
                "oS0", "oS1", "orr", "om", "oe0", "oe1", "oT0", "oT1", "oc0", "oc1", "ol", "oO", "oZ",
-               "sr", "sm", "sO", "slr", "sl", "sF", "rt", "ra", "rD", "rs", "rL", "rr", "ry", "st"]
+               "sr", "sm", "sO", "slr", "sF", "rt", "ra", "rD", "rs", "rL", "rr", "ry", "st"]
               + ["sS%d" % c for c in range(KB)] + ["se%d" % c for c in range(KB)]
               + ["sT%d" % c for c in range(KB)] + ["sc%d" % c for c in range(KB)])
 
@@ -47,23 +48,23 @@ def rank_program(g, core, T, topo):
     def engines(mask):
         return bin(mask).count("1")
 
-    sp.dma_start(T.qo[:], T.q[:]).then_inc(S.lq, 16)
     sp.dma_start(T.kk[:], T.k[:]).then_inc(S.lk, 16)
+    sp.dma_start(T.qo[:], T.q[:]).then_inc(S.lq, 16)
     sp.dma_start(T.vv[:], T.v[:]).then_inc(S.lv, 16)
 
     dve.memset(T.zer[:], 0.0).then_inc(S.z, 1)
-    if nxt is not None:
-        dve.memset(T.msg[:, QP:MW], 0.0).then_inc(S.mz, 1)
     g.wait_ge(S.z, 1)
     g.affine_select(T.negbig[:], T.zer[:], [[-1, 128]], AluOpType.is_equal, -30000.0, 0, 1).then_inc(S.nb, 1)
     act.wait_ge(S.nb, 1)
     act.activation(T.idn[:], T.negbig[:], Exp).then_inc(S.idr, 1)
 
-    if prev is not None:
-        rid, pid = topo.addr(prev, core)
-        mq = topo.mask(core, prev)
-        g.wait_ge(S.lq, 16)
-        g.remote_dma(T.qn[:], T.qo[:], S.qarr, S.qsent, pid, rid, mq)
+    if nxt is not None:
+        rid, pid = topo.addr(nxt, core)
+        mk = topo.mask(core, nxt)
+        g.wait_ge(S.lk, 16)
+        g.remote_dma(T.kn[:], T.kk[:], S.karr, S.ksent, pid, rid, mk)
+        g.wait_ge(S.lv, 16)
+        g.remote_dma(T.vn[:], T.vv[:], S.varr, S.vsent, pid, rid, mk)
 
     H = KB * BK // 2
     pe.wait_ge(S.lq, 16)
@@ -93,54 +94,6 @@ def rank_program(g, core, T, topo):
     dve.tensor_reduce(T.lo[Q, :], T.l2o[Q, :], X, AluOpType.add).then_inc(S.ol, 1)
     dve.wait_ge(S.oT1, 2)
     dve.tensor_copy(T.pto[:, 2 * QP:4 * QP], bank[6][:, 0:2 * QP]).then_inc(S.oc1, 1)
-
-    if nxt is not None:
-        rid, pid = topo.addr(nxt, core)
-        mr = topo.mask(core, nxt)
-        pe.wait_ge(S.qarr, engines(topo.mask(nxt, core)))
-        for c in range(KB):
-            pe.matmul(bank[c][Q, 0:BK], T.qn[:], T.kk[:, c * BK:(c + 1) * BK], True, True).then_inc(S["sS%d" % c], 1)
-        for c in range(KB):
-            dve.wait_ge(S["sS%d" % c], 1)
-            dve.tensor_reduce(T.nms[Q, c:c + 1], bank[c][Q, 0:BK], X, AluOpType.max, negate=True).then_inc(S.sr, 1)
-        dve.wait_ge(S.sr, KB)
-        dve.wait_ge(S.mz, 1)
-        dve.tensor_reduce(T.msg[Q, QP + 1:QP + 2], T.nms[Q, :], X, AluOpType.min).then_inc(S.sm, 1)
-        act.wait_ge(S.sm, 1)
-        for c in range(KB):
-            act.activation(T.ps[Q, c * BK:(c + 1) * BK], bank[c][Q, 0:BK], Exp, bias=T.msg[Q, QP + 1:QP + 2], scale=1.0,
-                           accum_out=T.l4s[Q, c:c + 1]).then_inc(S["se%d" % c], 1)
-
-        def turn(c):
-            pe.wait_ge(S["se%d" % c], 1)
-            pe.matmul(bank[c][:, 0:QP], T.ps[Q, c * BK:(c + 1) * BK], T.idn[Q, Q], True, True).then_inc(S["sT%d" % c], 1)
-
-        def pv(c):
-            pe.wait_ge(S["sc%d" % c], 1)
-            i = pe.matmul(bank[4][:, 0:QP], T.vv[:, c * BK:(c + 1) * BK], T.pts[:, c * QP:(c + 1) * QP], c == 0, c == KB - 1)
-            if c == KB - 1:
-                i.then_inc(S.sO, 1)
-
-        pe.wait_ge(S.lv, 16)
-        turn(0)
-        for c in range(1, KB):
-            turn(c)
-            pv(c - 1)
-        pv(KB - 1)
-        for c in range(KB):
-            if c == KB - 1:
-                dve.wait_ge(S["se%d" % c], 1)
-                dve.tensor_reduce(T.lfs[Q, :], T.l4s[Q, :], X, AluOpType.add).then_inc(S.slr, 1)
-            dve.wait_ge(S["sT%d" % c], 1)
-            dve.tensor_copy(T.pts[:, c * QP:(c + 1) * QP], bank[c][:, 0:QP]).then_inc(S["sc%d" % c], 1)
-        dve.wait_ge(S.slr, 1)
-        dve.tensor_copy(T.msg[Q, QP:QP + 1], T.lfs[Q, :]).then_inc(S.sl, 1)
-        dve.wait_ge(S.sO, 1)
-        dve.tensor_copy(T.msg[:, 0:QP], bank[4][:, 0:QP]).then_inc(S.sF, 1)
-        g.wait_ge(S.sl, 1)
-        g.wait_ge(S.sF, 1)
-        g.remote_dma(T.ret[:], T.msg[:], S.rarr, S.rsent, pid, rid, mr)
-
     pe.wait_ge(S.lv, 16)
     pe.wait_ge(S.oc0, 1)
     pe.wait_ge(S.oc1, 1)
@@ -158,21 +111,62 @@ def rank_program(g, core, T, topo):
         dve.wait_ge(S.oO, 1)
         dve.tensor_copy(T.zo[Q, :], bank[7][Q, 0:128]).then_inc(S.oZ, 1)
         na = engines(topo.mask(prev, core))
-        pe.wait_ge(S.rarr, na)
-        pe.matmul(bank[5][Q, 0:128], T.ret[:, 0:QP], T.idn[:], True, False)
-        dve.wait_ge(S.rarr, na)
-        dve.tensor_scalar(T.t1[Q, :], T.ret[Q, QP + 1:QP + 2], T.negmo[Q, :], CLAMP,
+        pe.wait_ge(S.karr, na)
+        for c in range(KB):
+            pe.matmul(bank[c][Q, 0:BK], T.qo[:], T.kn[:, c * BK:(c + 1) * BK], True, True).then_inc(S["sS%d" % c], 1)
+        for c in range(KB):
+            dve.wait_ge(S["sS%d" % c], 1)
+            dve.tensor_reduce(T.nms[Q, c:c + 1], bank[c][Q, 0:BK], X, AluOpType.max, negate=True).then_inc(S.sr, 1)
+        dve.wait_ge(S.sr, KB)
+        dve.tensor_reduce(T.negms[Q, :], T.nms[Q, :], X, AluOpType.min).then_inc(S.sm, 1)
+        dve.wait_ge(S.sm, 1)
+        dve.tensor_scalar(T.t1[Q, :], T.negms[Q, :], T.negmo[Q, :], CLAMP,
                           AluOpType.subtract, AluOpType.min).then_inc(S.rt, 1)
+        act.wait_ge(S.sm, 1)
+        for c in range(KB):
+            act.activation(T.ps[Q, c * BK:(c + 1) * BK], bank[c][Q, 0:BK], Exp, bias=T.negms[Q, :], scale=1.0,
+                           accum_out=T.l4s[Q, c:c + 1]).then_inc(S["se%d" % c], 1)
         act.wait_ge(S.rt, 1)
         act.activation(T.al[Q, :], T.t1[Q, :], Exp).then_inc(S.ra, 1)
         act.activation(T.da[Q, :], T.negbig[Q, Q], Exp, bias=T.t1[Q, :], scale=1.0).then_inc(S.rD, 1)
+
+        def turn(c):
+            pe.wait_ge(S["se%d" % c], 1)
+            pe.matmul(bank[c][:, 0:QP], T.ps[Q, c * BK:(c + 1) * BK], T.idn[Q, Q], True, True).then_inc(S["sT%d" % c], 1)
+
+        def pv(c):
+            pe.wait_ge(S["sc%d" % c], 1)
+            j = pe.matmul(bank[4][:, 0:QP], T.vn[:, c * BK:(c + 1) * BK], T.pts[:, c * QP:(c + 1) * QP], c == 0, c == KB - 1)
+            if c == KB - 1:
+                j.then_inc(S.sO, 1)
+
+        turn(0)
+        turn(1)
+        pe.wait_ge(S.varr, na)
+        pv(0)
+        for c in range(2, KB):
+            turn(c)
+            pv(c - 1)
+        pv(KB - 1)
         pe.wait_ge(S.rD, 1)
         pe.wait_ge(S.oZ, 1)
-        pe.matmul(bank[5][Q, 0:128], T.da[Q, :], T.zo[Q, :], False, True).then_inc(S.rs, 1)
+        pe.matmul(bank[5][Q, 0:128], T.da[Q, :], T.zo[Q, :], True, False)
+        pe.wait_ge(S.sF, 1)
+        pe.matmul(bank[5][Q, 0:128], T.ot[:], T.idn[:], False, True).then_inc(S.rs, 1)
+
+        for c in range(KB):
+            if c == KB - 1:
+                dve.wait_ge(S["se%d" % c], 1)
+                dve.tensor_reduce(T.lfs[Q, :], T.l4s[Q, :], X, AluOpType.add).then_inc(S.slr, 1)
+            dve.wait_ge(S["sT%d" % c], 1)
+            dve.tensor_copy(T.pts[:, c * QP:(c + 1) * QP], bank[c][:, 0:QP]).then_inc(S["sc%d" % c], 1)
+        dve.wait_ge(S.slr, 1)
         dve.wait_ge(S.ra, 1)
         dve.wait_ge(S.ol, 1)
-        dve.tensor_scalar(T.lsum[Q, :], T.lo[Q, :], T.al[Q, :], T.ret[Q, QP:QP + 1],
+        dve.tensor_scalar(T.lsum[Q, :], T.lo[Q, :], T.al[Q, :], T.lfs[Q, :],
                           AluOpType.mult, AluOpType.add).then_inc(S.rL, 1)
+        dve.wait_ge(S.sO, 1)
+        dve.tensor_copy(T.ot[:], bank[4][:, 0:QP]).then_inc(S.sF, 1)
         dve.wait_ge(S.rL, 1)
         dve.reciprocal(T.rec[Q, :], T.lsum[Q, :]).then_inc(S.rr, 1)
         dve.wait_ge(S.rr, 1)
@@ -182,7 +176,6 @@ def rank_program(g, core, T, topo):
     sp.wait_ge(S.ry, 1)
     sp.dma_start(T.y[:], T.yb[Q, :]).then_inc(S.st, 16)
     sp.wait_ge(S.st, 16)
-    if prev is not None:
-        g.wait_ge(S.qsent, engines(topo.mask(core, prev)))
     if nxt is not None:
-        g.wait_ge(S.rsent, engines(topo.mask(core, nxt)))
+        g.wait_ge(S.ksent, engines(topo.mask(core, nxt)))
+        g.wait_ge(S.vsent, engines(topo.mask(core, nxt)))

from concourse.mybir import AluOpType, AxisListType, ActivationFunctionType

QP, KB, BK = 64, 4, 128
CLAMP = 60.0

SCRATCH = {
    "qo": ("sbuf", [128, QP], "bfloat16"),
    "kk": ("sbuf", [128, KB * BK], "bfloat16"), "vv": ("sbuf", [128, KB * BK], "bfloat16"),
    "kn": ("sbuf", [128, KB * BK], "bfloat16"), "vn": ("sbuf", [128, KB * BK], "bfloat16"),
    "zer": ("sbuf", [128, 128], "float32"), "negbig": ("sbuf", [128, 128], "float32"),
    "idn": ("sbuf", [128, 128], "bfloat16"),
    "nmo": ("sbuf", [128, 2], "float32"), "negmo": ("sbuf", [128, 1], "bfloat16"),
    "po": ("sbuf", [128, KB * BK], "bfloat16"), "l2o": ("sbuf", [128, 2], "float32"),
    "lo": ("sbuf", [128, 1], "float32"), "pto": ("sbuf", [128, KB * QP], "bfloat16"),
    "zo": ("sbuf", [128, 128], "bfloat16"),
    "nms": ("sbuf", [128, KB], "float32"), "negms": ("sbuf", [128, 1], "bfloat16"),
    "ps": ("sbuf", [128, KB * BK], "bfloat16"),
    "l4s": ("sbuf", [128, KB], "float32"), "lfs": ("sbuf", [128, 1], "float32"),
    "pts": ("sbuf", [128, KB * QP], "bfloat16"), "ot": ("sbuf", [128, QP], "bfloat16"),
    "t1": ("sbuf", [128, 1], "float32"),
    "al": ("sbuf", [128, 1], "float32"), "da": ("sbuf", [128, QP], "bfloat16"),
    "lsum": ("sbuf", [128, 1], "float32"), "rec": ("sbuf", [128, 1], "float32"),
    "yb": ("sbuf", [128, 128], "bfloat16"),
}
for _b in range(8):
    SCRATCH["b%d" % _b] = ("psum", [128, 512], "float32")

SEMAPHORES = (["z", "nb", "idr", "lq", "lk", "lv", "karr", "varr", "ksent", "vsent",
               "oS0", "oS1", "orr", "om", "oe0", "oe1", "oT0", "oT1", "oc0", "oc1", "ol", "oO", "oZ",
               "sr", "sm", "sO", "slr", "sF", "rt", "ra", "rD", "rs", "rL", "rr", "ry", "st"]
              + ["sS%d" % c for c in range(KB)] + ["se%d" % c for c in range(KB)]
              + ["sT%d" % c for c in range(KB)] + ["sc%d" % c for c in range(KB)])


def rank_program(g, core, T, topo):
    r = T.rank_of(core)
    if r is None:
        return
    prev = T.cores[r - 1] if r > 0 else None
    nxt = T.cores[r + 1] if r + 1 < len(T.cores) else None
    S = T.sem
    pe, dve, act, sp = g.tensor, g.vector, g.scalar, g.sync
    Exp = ActivationFunctionType.Exp
    X = AxisListType.X
    Q = slice(0, QP)
    bank = [T["b%d" % b] for b in range(8)]

    def engines(mask):
        return bin(mask).count("1")

    sp.dma_start(T.kk[:], T.k[:]).then_inc(S.lk, 16)
    sp.dma_start(T.qo[:], T.q[:]).then_inc(S.lq, 16)
    sp.dma_start(T.vv[:], T.v[:]).then_inc(S.lv, 16)

    dve.memset(T.zer[:], 0.0).then_inc(S.z, 1)
    g.wait_ge(S.z, 1)
    g.affine_select(T.negbig[:], T.zer[:], [[-1, 128]], AluOpType.is_equal, -30000.0, 0, 1).then_inc(S.nb, 1)
    act.wait_ge(S.nb, 1)
    act.activation(T.idn[:], T.negbig[:], Exp).then_inc(S.idr, 1)

    if nxt is not None:
        rid, pid = topo.addr(nxt, core)
        mk = topo.mask(core, nxt)
        g.wait_ge(S.lk, 16)
        g.remote_dma(T.kn[:], T.kk[:], S.karr, S.ksent, pid, rid, mk)
        g.wait_ge(S.lv, 16)
        g.remote_dma(T.vn[:], T.vv[:], S.varr, S.vsent, pid, rid, mk)

    H = KB * BK // 2
    pe.wait_ge(S.lq, 16)
    pe.wait_ge(S.lk, 16)
    for c in range(2):
        pe.matmul(bank[5 + c][Q, 0:H], T.qo[:], T.kk[:, c * H:(c + 1) * H], True, True).then_inc(S["oS%d" % c], 1)
    for c in range(2):
        dve.wait_ge(S["oS%d" % c], 1)
        dve.tensor_reduce(T.nmo[Q, c:c + 1], bank[5 + c][Q, 0:H], X, AluOpType.max, negate=True).then_inc(S.orr, 1)
    dve.wait_ge(S.orr, 2)
    dve.tensor_reduce(T.negmo[Q, :], T.nmo[Q, :], X, AluOpType.min).then_inc(S.om, 1)
    act.wait_ge(S.om, 1)
    for c in range(2):
        act.activation(T.po[Q, c * H:(c + 1) * H], bank[5 + c][Q, 0:H], Exp, bias=T.negmo[Q, :], scale=1.0,
                       accum_out=T.l2o[Q, c:c + 1]).then_inc(S["oe%d" % c], 1)
    pe.wait_ge(S.idr, 1)
    for c in range(2):
        pe.wait_ge(S["oe%d" % c], 1)
        for h in range(2):
            b = 2 * c + h
            pe.matmul(bank[5 + c][:, h * QP:(h + 1) * QP], T.po[Q, b * BK:(b + 1) * BK], T.idn[Q, Q],
                      True, True).then_inc(S["oT%d" % c], 1)
    dve.wait_ge(S.oT0, 2)
    dve.tensor_copy(T.pto[:, 0:2 * QP], bank[5][:, 0:2 * QP]).then_inc(S.oc0, 1)
    dve.wait_ge(S.oe0, 1)
    dve.wait_ge(S.oe1, 1)
    dve.tensor_reduce(T.lo[Q, :], T.l2o[Q, :], X, AluOpType.add).then_inc(S.ol, 1)
    dve.wait_ge(S.oT1, 2)
    dve.tensor_copy(T.pto[:, 2 * QP:4 * QP], bank[6][:, 0:2 * QP]).then_inc(S.oc1, 1)
    pe.wait_ge(S.lv, 16)
    pe.wait_ge(S.oc0, 1)
    pe.wait_ge(S.oc1, 1)
    for b in range(KB):
        i = pe.matmul(bank[7][Q, 0:128], T.pto[:, b * QP:(b + 1) * QP], T.vv[:, b * BK:(b + 1) * BK], b == 0, b == KB - 1)
    i.then_inc(S.oO, 1)

    if prev is None:
        dve.wait_ge(S.ol, 1)
        dve.reciprocal(T.rec[Q, :], T.lo[Q, :]).then_inc(S.rr, 1)
        dve.wait_ge(S.rr, 1)
        dve.wait_ge(S.oO, 1)
        dve.tensor_scalar(T.yb[Q, :], bank[7][Q, 0:128], T.rec[Q, :], None, AluOpType.mult).then_inc(S.ry, 1)
    else:
        dve.wait_ge(S.oO, 1)
        dve.tensor_copy(T.zo[Q, :], bank[7][Q, 0:128]).then_inc(S.oZ, 1)
        na = engines(topo.mask(prev, core))
        pe.wait_ge(S.karr, na)
        for c in range(KB):
            pe.matmul(bank[c][Q, 0:BK], T.qo[:], T.kn[:, c * BK:(c + 1) * BK], True, True).then_inc(S["sS%d" % c], 1)
        for c in range(KB):
            dve.wait_ge(S["sS%d" % c], 1)
            dve.tensor_reduce(T.nms[Q, c:c + 1], bank[c][Q, 0:BK], X, AluOpType.max, negate=True).then_inc(S.sr, 1)
        dve.wait_ge(S.sr, KB)
        dve.tensor_reduce(T.negms[Q, :], T.nms[Q, :], X, AluOpType.min).then_inc(S.sm, 1)
        dve.wait_ge(S.sm, 1)
        dve.tensor_scalar(T.t1[Q, :], T.negms[Q, :], T.negmo[Q, :], CLAMP,
                          AluOpType.subtract, AluOpType.min).then_inc(S.rt, 1)
        act.wait_ge(S.sm, 1)
        for c in range(KB):
            act.activation(T.ps[Q, c * BK:(c + 1) * BK], bank[c][Q, 0:BK], Exp, bias=T.negms[Q, :], scale=1.0,
                           accum_out=T.l4s[Q, c:c + 1]).then_inc(S["se%d" % c], 1)
        act.wait_ge(S.rt, 1)
        act.activation(T.al[Q, :], T.t1[Q, :], Exp).then_inc(S.ra, 1)
        act.activation(T.da[Q, :], T.negbig[Q, Q], Exp, bias=T.t1[Q, :], scale=1.0).then_inc(S.rD, 1)

        def turn(c):
            pe.wait_ge(S["se%d" % c], 1)
            pe.matmul(bank[c][:, 0:QP], T.ps[Q, c * BK:(c + 1) * BK], T.idn[Q, Q], True, True).then_inc(S["sT%d" % c], 1)

        def pv(c):
            pe.wait_ge(S["sc%d" % c], 1)
            j = pe.matmul(bank[4][:, 0:QP], T.vn[:, c * BK:(c + 1) * BK], T.pts[:, c * QP:(c + 1) * QP], c == 0, c == KB - 1)
            if c == KB - 1:
                j.then_inc(S.sO, 1)

        turn(0)
        turn(1)
        pe.wait_ge(S.varr, na)
        pv(0)
        for c in range(2, KB):
            turn(c)
            pv(c - 1)
        pv(KB - 1)
        pe.wait_ge(S.rD, 1)
        pe.wait_ge(S.oZ, 1)
        pe.matmul(bank[5][Q, 0:128], T.da[Q, :], T.zo[Q, :], True, False)
        pe.wait_ge(S.sF, 1)
        pe.matmul(bank[5][Q, 0:128], T.ot[:], T.idn[:], False, True).then_inc(S.rs, 1)

        for c in range(KB):
            if c == KB - 1:
                dve.wait_ge(S["se%d" % c], 1)
                dve.tensor_reduce(T.lfs[Q, :], T.l4s[Q, :], X, AluOpType.add).then_inc(S.slr, 1)
            dve.wait_ge(S["sT%d" % c], 1)
            dve.tensor_copy(T.pts[:, c * QP:(c + 1) * QP], bank[c][:, 0:QP]).then_inc(S["sc%d" % c], 1)
        dve.wait_ge(S.slr, 1)
        dve.wait_ge(S.ra, 1)
        dve.wait_ge(S.ol, 1)
        dve.tensor_scalar(T.lsum[Q, :], T.lo[Q, :], T.al[Q, :], T.lfs[Q, :],
                          AluOpType.mult, AluOpType.add).then_inc(S.rL, 1)
        dve.wait_ge(S.sO, 1)
        dve.tensor_copy(T.ot[:], bank[4][:, 0:QP]).then_inc(S.sF, 1)
        dve.wait_ge(S.rL, 1)
        dve.reciprocal(T.rec[Q, :], T.lsum[Q, :]).then_inc(S.rr, 1)
        dve.wait_ge(S.rr, 1)
        dve.wait_ge(S.rs, 1)
        dve.tensor_scalar(T.yb[Q, :], bank[5][Q, 0:128], T.rec[Q, :], None, AluOpType.mult).then_inc(S.ry, 1)

    sp.wait_ge(S.ry, 1)
    sp.dma_start(T.y[:], T.yb[Q, :]).then_inc(S.st, 16)
    sp.wait_ge(S.st, 16)
    if nxt is not None:
        g.wait_ge(S.ksent, engines(topo.mask(core, nxt)))
        g.wait_ge(S.vsent, engines(topo.mask(core, nxt)))
